import numpy as np
import ml_dtypes

BF16 = ml_dtypes.bfloat16


def bf(x):
    return np.asarray(x, np.float32).astype(BF16)


def f32(x):
    return np.asarray(x, np.float32)


def f64(x):
    return np.asarray(x).astype(np.float64)


def striped(idx):
    return np.tile(idx.reshape(-1, 16).T, (8, 1))


S, K, M, N, D, V = 512, 128, 256, 192, 3, 64


def setup_inputs():
    return {"table": bf(np.random.standard_normal((K, S))), "w": bf(np.random.standard_normal((D, K, M)) / np.sqrt(D * K)), "b": f32(0.5 * np.random.standard_normal((M, 1))), "offs": striped(np.random.permutation(S)[:N])}


def reference(table, w, b, offs):
    idx = offs[:16].T.reshape(-1)
    x = f64(table)[:, idx]
    y = sum(f64(w)[t].T @ x[:, t * V : (t + 1) * V] for t in range(D))
    return y + f64(b)

@@ -1,0 +1,45 @@
+import concourse.mybir as mybir
+
+BF16, F32, U16 = mybir.dt.bfloat16, mybir.dt.float32, mybir.dt.uint16
+
+P = 128
+S = 512
+M = 256
+RELATIONS = 3
+NODES = 64
+BLOCKS = M // P
+PIECE_COLUMNS = NODES // 16
+
+FLOPS = 2 * P * M * RELATIONS * NODES
+
+
+def tile_gather_matmul_kernel(tc, table, w, b, offs, out):
+    nc = tc.nc
+    with (
+        tc.tile_pool(name="held", bufs=1) as held,
+        tc.psum_pool(name="psum", bufs=1) as psum,
+    ):
+        offsets = held.tile([P, RELATIONS * PIECE_COLUMNS], U16, name="offsets")
+        nc.sync.dma_start(offsets[:], offs)
+        nodes = held.tile([P, S], BF16, name="nodes")
+        nc.sync.dma_start(nodes[:], table)
+        weights = held.tile([P, RELATIONS, M], BF16, name="weights")
+        nc.scalar.dma_start(weights[:], w.rearrange("t k m -> k t m"))
+        bias = held.tile([P, BLOCKS], F32, name="bias")
+        nc.scalar.dma_start(bias[:], b.rearrange("(a p) o -> p (a o)", p=P))
+
+        for a in range(BLOCKS):
+            sums = psum.tile([P, NODES], F32, name=f"sums{a}")
+            for t in range(RELATIONS):
+                neighbours = nodes[:].indirect(offsets[:, t * PIECE_COLUMNS : (t + 1) * PIECE_COLUMNS])
+                nc.tensor.matmul(
+                    sums[:],
+                    weights[:, t, a * P : (a + 1) * P],
+                    neighbours,
+                    start=(t == 0),
+                    stop=(t == RELATIONS - 1),
+                )
+            y = held.tile([P, NODES], F32, name=f"y{a}")
+            nc.vector.tensor_scalar_add(y[:], sums[:], bias[:, a : a + 1])
+            store_queue = nc.sync if a % 2 == 0 else nc.scalar
+            store_queue.dma_start(out[a * P : (a + 1) * P, :], y[:])

@@ -23,23 +23,26 @@ def tile_gather_matmul_kernel(tc, table, w, b, offs, out):
         nc.sync.dma_start(offsets[:], offs)
         nodes = held.tile([P, S], BF16, name="nodes")
         nc.sync.dma_start(nodes[:], table)
-        weights = held.tile([P, RELATIONS, M], BF16, name="weights")
-        nc.scalar.dma_start(weights[:], w.rearrange("t k m -> k t m"))
+        weights = [held.tile([P, M], BF16, name=f"weights{t}") for t in range(RELATIONS)]
+        for t in range(RELATIONS):
+            nc.scalar.dma_start(weights[t][:], w[t])
         bias = held.tile([P, BLOCKS], F32, name="bias")
         nc.scalar.dma_start(bias[:], b.rearrange("(a p) o -> p (a o)", p=P))
 
-        for a in range(BLOCKS):
-            sums = psum.tile([P, NODES], F32, name=f"sums{a}")
-            for t in range(RELATIONS):
-                neighbours = nodes[:].indirect(offsets[:, t * PIECE_COLUMNS : (t + 1) * PIECE_COLUMNS])
+        sums = [psum.tile([P, NODES], F32, name=f"sums{a}") for a in range(BLOCKS)]
+        for t in range(RELATIONS):
+            neighbours = nodes[:].indirect(offsets[:, t * PIECE_COLUMNS : (t + 1) * PIECE_COLUMNS])
+            for a in range(BLOCKS):
                 nc.tensor.matmul(
-                    sums[:],
-                    weights[:, t, a * P : (a + 1) * P],
+                    sums[a][:],
+                    weights[t][:, a * P : (a + 1) * P],
                     neighbours,
                     start=(t == 0),
                     stop=(t == RELATIONS - 1),
                 )
+
+        for a in range(BLOCKS):
             y = held.tile([P, NODES], F32, name=f"y{a}")
-            nc.vector.tensor_scalar_add(y[:], sums[:], bias[:, a : a + 1])
-            store_queue = nc.sync if a % 2 == 0 else nc.scalar
+            nc.vector.tensor_scalar_add(y[:], sums[a][:], bias[:, a : a + 1])
+            store_queue = nc.sync if a == BLOCKS - 1 else nc.scalar
             store_queue.dma_start(out[a * P : (a + 1) * P, :], y[:])

@@ -9,6 +9,8 @@ RELATIONS = 3
 NODES = 64
 BLOCKS = M // P
 PIECE_COLUMNS = NODES // 16
+BANK = 512
+WARM_UP_MATMULS = 4
 
 FLOPS = 2 * P * M * RELATIONS * NODES
 
@@ -23,26 +25,29 @@ def tile_gather_matmul_kernel(tc, table, w, b, offs, out):
         nc.sync.dma_start(offsets[:], offs)
         nodes = held.tile([P, S], BF16, name="nodes")
         nc.sync.dma_start(nodes[:], table)
-        weights = [held.tile([P, M], BF16, name=f"weights{t}") for t in range(RELATIONS)]
-        for t in range(RELATIONS):
-            nc.scalar.dma_start(weights[t][:], w[t])
+        weights = held.tile([P, RELATIONS, M], BF16, name="weights")
+        nc.scalar.dma_start(weights[:], w.rearrange("t k m -> k t m"))
         bias = held.tile([P, BLOCKS], F32, name="bias")
         nc.scalar.dma_start(bias[:], b.rearrange("(a p) o -> p (a o)", p=P))
 
-        sums = [psum.tile([P, NODES], F32, name=f"sums{a}") for a in range(BLOCKS)]
-        for t in range(RELATIONS):
-            neighbours = nodes[:].indirect(offsets[:, t * PIECE_COLUMNS : (t + 1) * PIECE_COLUMNS])
-            for a in range(BLOCKS):
+        zeros = held.tile([P, BANK], BF16, name="zeros")
+        nc.vector.memset(zeros[:], 0.0)
+        unread = psum.tile([P, BANK], F32, name="unread")
+        for i in range(WARM_UP_MATMULS):
+            nc.tensor.matmul(unread[:], zeros[:, 0:P], zeros[:], start=True, stop=True)
+
+        for a in range(BLOCKS):
+            sums = psum.tile([P, NODES], F32, name=f"sums{a}")
+            for t in range(RELATIONS):
+                neighbours = nodes[:].indirect(offsets[:, t * PIECE_COLUMNS : (t + 1) * PIECE_COLUMNS])
                 nc.tensor.matmul(
-                    sums[a][:],
-                    weights[t][:, a * P : (a + 1) * P],
+                    sums[:],
+                    weights[:, t, a * P : (a + 1) * P],
                     neighbours,
                     start=(t == 0),
                     stop=(t == RELATIONS - 1),
                 )
-
-        for a in range(BLOCKS):
             y = held.tile([P, NODES], F32, name=f"y{a}")
-            nc.vector.tensor_scalar_add(y[:], sums[a][:], bias[:, a : a + 1])
-            store_queue = nc.sync if a == BLOCKS - 1 else nc.scalar
+            nc.vector.tensor_scalar_add(y[:], sums[:], bias[:, a : a + 1])
+            store_queue = nc.sync if a % 2 == 0 else nc.scalar
             store_queue.dma_start(out[a * P : (a + 1) * P, :], y[:])

@@ -26,7 +26,7 @@ def tile_gather_matmul_kernel(tc, table, w, b, offs, out):
         nodes = held.tile([P, S], BF16, name="nodes")
         nc.sync.dma_start(nodes[:], table)
         weights = held.tile([P, RELATIONS, M], BF16, name="weights")
-        nc.scalar.dma_start(weights[:], w.rearrange("t k m -> k t m"))
+        nc.sync.dma_start(weights[:], w.rearrange("t k m -> k t m"))
         bias = held.tile([P, BLOCKS], F32, name="bias")
         nc.scalar.dma_start(bias[:], b.rearrange("(a p) o -> p (a o)", p=P))
 

@@ -25,8 +25,9 @@ def tile_gather_matmul_kernel(tc, table, w, b, offs, out):
         nc.sync.dma_start(offsets[:], offs)
         nodes = held.tile([P, S], BF16, name="nodes")
         nc.sync.dma_start(nodes[:], table)
-        weights = held.tile([P, RELATIONS, M], BF16, name="weights")
-        nc.sync.dma_start(weights[:], w.rearrange("t k m -> k t m"))
+        weights = [held.tile([P, M], BF16, name=f"weights{t}") for t in range(RELATIONS)]
+        for t in range(RELATIONS):
+            nc.sync.dma_start(weights[t][:], w[t])
         bias = held.tile([P, BLOCKS], F32, name="bias")
         nc.scalar.dma_start(bias[:], b.rearrange("(a p) o -> p (a o)", p=P))
 
@@ -36,18 +37,19 @@ def tile_gather_matmul_kernel(tc, table, w, b, offs, out):
         for i in range(WARM_UP_MATMULS):
             nc.tensor.matmul(unread[:], zeros[:, 0:P], zeros[:], start=True, stop=True)
 
-        for a in range(BLOCKS):
-            sums = psum.tile([P, NODES], F32, name=f"sums{a}")
-            for t in range(RELATIONS):
+        sums = [psum.tile([P, NODES], F32, name=f"sums{a}") for a in range(BLOCKS)]
+        for t in range(RELATIONS):
+            for a in range(BLOCKS):
                 neighbours = nodes[:].indirect(offsets[:, t * PIECE_COLUMNS : (t + 1) * PIECE_COLUMNS])
                 nc.tensor.matmul(
-                    sums[:],
-                    weights[:, t, a * P : (a + 1) * P],
+                    sums[a][:],
+                    weights[t][:, a * P : (a + 1) * P],
                     neighbours,
                     start=(t == 0),
                     stop=(t == RELATIONS - 1),
                 )
+        for a in range(BLOCKS):
             y = held.tile([P, NODES], F32, name=f"y{a}")
-            nc.vector.tensor_scalar_add(y[:], sums[:], bias[:, a : a + 1])
+            nc.vector.tensor_scalar_add(y[:], sums[a][:], bias[:, a : a + 1])
             store_queue = nc.sync if a % 2 == 0 else nc.scalar
             store_queue.dma_start(out[a * P : (a + 1) * P, :], y[:])

@@ -21,10 +21,10 @@ def tile_gather_matmul_kernel(tc, table, w, b, offs, out):
         tc.tile_pool(name="held", bufs=1) as held,
         tc.psum_pool(name="psum", bufs=1) as psum,
     ):
-        offsets = held.tile([P, RELATIONS * PIECE_COLUMNS], U16, name="offsets")
-        nc.sync.dma_start(offsets[:], offs)
         nodes = held.tile([P, S], BF16, name="nodes")
         nc.sync.dma_start(nodes[:], table)
+        offsets = held.tile([P, RELATIONS * PIECE_COLUMNS], U16, name="offsets")
+        nc.sync.dma_start(offsets[:], offs)
         weights = [held.tile([P, M], BF16, name=f"weights{t}") for t in range(RELATIONS)]
         for t in range(RELATIONS):
             nc.sync.dma_start(weights[t][:], w[t])

import concourse.mybir as mybir

BF16, F32, U16 = mybir.dt.bfloat16, mybir.dt.float32, mybir.dt.uint16

P = 128
S = 512
M = 256
RELATIONS = 3
NODES = 64
BLOCKS = M // P
PIECE_COLUMNS = NODES // 16
BANK = 512
WARM_UP_MATMULS = 4

FLOPS = 2 * P * M * RELATIONS * NODES


def tile_gather_matmul_kernel(tc, table, w, b, offs, out):
    nc = tc.nc
    with (
        tc.tile_pool(name="held", bufs=1) as held,
        tc.psum_pool(name="psum", bufs=1) as psum,
    ):
        nodes = held.tile([P, S], BF16, name="nodes")
        nc.sync.dma_start(nodes[:], table)
        offsets = held.tile([P, RELATIONS * PIECE_COLUMNS], U16, name="offsets")
        nc.sync.dma_start(offsets[:], offs)
        weights = [held.tile([P, M], BF16, name=f"weights{t}") for t in range(RELATIONS)]
        for t in range(RELATIONS):
            nc.sync.dma_start(weights[t][:], w[t])
        bias = held.tile([P, BLOCKS], F32, name="bias")
        nc.scalar.dma_start(bias[:], b.rearrange("(a p) o -> p (a o)", p=P))

        zeros = held.tile([P, BANK], BF16, name="zeros")
        nc.vector.memset(zeros[:], 0.0)
        unread = psum.tile([P, BANK], F32, name="unread")
        for i in range(WARM_UP_MATMULS):
            nc.tensor.matmul(unread[:], zeros[:, 0:P], zeros[:], start=True, stop=True)

        sums = [psum.tile([P, NODES], F32, name=f"sums{a}") for a in range(BLOCKS)]
        for t in range(RELATIONS):
            for a in range(BLOCKS):
                neighbours = nodes[:].indirect(offsets[:, t * PIECE_COLUMNS : (t + 1) * PIECE_COLUMNS])
                nc.tensor.matmul(
                    sums[a][:],
                    weights[t][:, a * P : (a + 1) * P],
                    neighbours,
                    start=(t == 0),
                    stop=(t == RELATIONS - 1),
                )
        for a in range(BLOCKS):
            y = held.tile([P, NODES], F32, name=f"y{a}")
            nc.vector.tensor_scalar_add(y[:], sums[a][:], bias[:, a : a + 1])
            store_queue = nc.sync if a % 2 == 0 else nc.scalar
            store_queue.dma_start(out[a * P : (a + 1) * P, :], y[:])
